import numpy as np
import ml_dtypes


def mxq(x, axis, fmt="e4m3"):
    dtype, down = {"e4m3": (ml_dtypes.float8_e4m3fn, 7), "e5m2": (ml_dtypes.float8_e5m2, 14)}[fmt]
    v = np.moveaxis(np.asarray(x, np.float32).astype(ml_dtypes.bfloat16).astype(np.float64), axis, -1)
    blocks = v.reshape(v.shape[:-1] + (-1, 32))
    amax = np.abs(blocks).max(-1, keepdims=True)
    byte = np.maximum(np.where(amax > 0, np.frexp(amax)[1] - 1 + 127, 0) - down, 1)
    scale = np.exp2(byte - 127.0)
    codes = (blocks / scale).astype(np.float32).astype(dtype).astype(np.float64)
    return np.moveaxis((codes * scale).reshape(v.shape), -1, axis)


WIDE = False


def mx_kscale(k):
    if not WIDE:
        return np.ones(k)
    levels = np.array([10, -10, 5, -5, 0])
    if k % 512:
        return np.exp2(np.random.permutation(np.resize(levels, k // 32))).repeat(32)
    a = np.empty((k // 512, 16))
    for p in range(k // 512):
        a[p, :8] = np.random.permutation(np.resize(levels, 8))
        for g in range(8):
            far = levels[np.abs(levels - a[p, g]) >= 10]
            a[p, g + 8] = far[np.random.randint(len(far))]
    return np.exp2(a.ravel()).repeat(32)


def f64(x):
    return np.asarray(x).astype(np.float64)


def striped8(idx):
    return np.asarray(idx).reshape(8, -1, 16).transpose(0, 2, 1).reshape(128, -1).astype(np.uint16)


def unstriped8(offs):
    return offs.reshape(8, 16, -1).transpose(0, 2, 1).reshape(8, -1).astype(np.int64)


def pick8(x, idx, run):
    r = np.arange(len(x))
    return x[r[:, None], idx[r % (8 * run) // run]]


E2M1 = np.array([0.0, 0.5, 1.0, 1.5, 2.0, 3.0, 4.0, 6.0, -0.0, -0.5, -1.0, -1.5, -2.0, -3.0, -4.0, -6.0])


def pack_weight(w, fmt):
    k, n = w.shape
    w = f64(np.asarray(w, np.float32).astype(ml_dtypes.bfloat16)).reshape(k // 32, 32, n)
    amax = np.abs(w).max(1)
    if fmt == "e4m3":
        byte = np.frexp(amax)[1] - 1 + 127 - 7
    else:
        mant, ex = np.frexp(amax / 6.0)
        byte = np.where(mant > 0.5, ex, ex - 1) + 127
    byte = np.clip(np.where(amax > 0, byte, 1), 1, 254)
    scaled = (w * np.exp2(127.0 - byte)[:, None, :]).reshape(k, n).astype(np.float32)
    by_word = np.ascontiguousarray(scaled.reshape(k // 512, 128, 4, n).transpose(0, 1, 3, 2))
    if fmt == "e4m3":
        words = by_word.astype(ml_dtypes.float8_e4m3fn).view(np.uint8)
    else:
        c = by_word.astype(ml_dtypes.float4_e2m1fn).view(np.uint8) & 0xF
        words = (c[..., 0::2] | (c[..., 1::2] << 4)).reshape(k // 512, 128, 2 * n)
    return np.ascontiguousarray(words), np.ascontiguousarray(byte.astype(np.uint8).reshape(k // 512, 16, n))


def unpack_weight(words, scales, fmt):
    g, _, n = scales.shape
    words = np.ascontiguousarray(words).reshape(g, 128, n, -1)
    if fmt == "e4m3":
        vals = words.view(ml_dtypes.float8_e4m3fn).astype(np.float64)
    else:
        nib = np.empty((g, 128, n, 4), np.uint8)
        nib[..., 0::2] = words & 0xF
        nib[..., 1::2] = words >> 4
        vals = E2M1[nib]
    vals = vals * np.repeat(np.exp2(scales.astype(np.float64) - 127.0), 8, axis=1)[..., None]
    return vals.transpose(0, 1, 3, 2).reshape(g * 512, n)


D, T, I, Q = 512, 1024, 512, 128


def setup_inputs():
    n = np.random.standard_normal
    idx = np.stack([np.random.permutation(T)[:I] for _ in range(8)])
    idx2 = np.stack([np.random.permutation(T)[:I] for _ in range(8)])
    idx3 = np.stack([np.random.permutation(T)[:I] for _ in range(8)])
    idx4 = np.stack([np.random.permutation(T)[:I] for _ in range(8)])
    fd = mx_kscale(D)
    keysp = pack_weight(n((D, T)) / fd[:, None], "e4m3")
    return {
        "query": (n((D, Q)) * 0.9 / np.sqrt(D) * fd[:, None]).astype(np.float32),
        "keys_words": keysp[0],
        "keys_scales": keysp[1],
        "lam": (np.random.uniform(0.3, 0.9, (Q, 1))).astype(np.float32),
        "old": (1.0 * n((Q, T))).astype(np.float32),
        "offs": striped8(idx),
        "offs2": striped8(idx2),
        "offs3": striped8(idx3),
        "offs4": striped8(idx4),
    }


def reference(query, keys_words, keys_scales, lam, old, offs, offs2, offs3, offs4):
    idx = unstriped8(offs)
    idx2 = unstriped8(offs2)
    idx3 = unstriped8(offs3)
    idx4 = unstriped8(offs4)
    keysu = unpack_weight(keys_words, keys_scales, "e4m3")
    queryq = mxq(f64(query), 0, "e4m3")
    a = queryq.T @ keysu
    w = pick8(a, idx, 16) + np.maximum(pick8(a, idx2, 16), pick8(a, idx3, 16)) * f64(lam)
    f1 = np.zeros((Q, T))
    f1[np.arange(Q)[:, None], idx[np.arange(Q) % 128 // 16]] = w
    f2 = f1 + f64(old)
    y = pick8(f2, idx4, 16)
    return y

@@ -1,0 +1,118 @@
+from contextlib import ExitStack
+
+import concourse.mybir as mybir
+
+D, T, I, Q = 512, 1024, 512, 128
+FLOPS = 2 * D * Q * T
+
+F32 = mybir.dt.float32
+BF16 = mybir.dt.bfloat16
+I32 = mybir.dt.int32
+U32 = mybir.dt.uint32
+U16 = mybir.dt.uint16
+U8 = mybir.dt.uint8
+FP8X4 = mybir.dt.float8_e4m3fn_x4
+ALU = mybir.AluOpType
+COPY = mybir.ActivationFunctionType.Copy
+
+P = 128
+PACK = 4
+LIST_COLS = I // 16
+
+
+def tile_attend_lookahead_lean_through_heads_kernel(tc, query, keys_words, keys_scales, lam, old, offs, offs2, offs3, offs4, out):
+    nc = tc.nc
+    half_t = T // 2
+    quarter_t = T // 4
+    half_i = I // 2
+    half_cols = LIST_COLS // 2
+
+    with ExitStack() as ctx:
+        lists = ctx.enter_context(tc.tile_pool(name="lists", bufs=1))
+        sb = ctx.enter_context(tc.tile_pool(name="sb", bufs=1))
+        psum = ctx.enter_context(tc.psum_pool(name="psum", bufs=1))
+
+        idx1 = lists.tile([P, LIST_COLS], U16, name="idx1")
+        idx2 = lists.tile([P, LIST_COLS], U16, name="idx2")
+        idx3 = lists.tile([P, LIST_COLS], U16, name="idx3")
+        idx4 = lists.tile([P, LIST_COLS], U16, name="idx4")
+
+        q_raw = sb.tile([P, PACK, Q], F32, name="q_raw")
+        nc.sync.dma_start(out=q_raw[:], in_=query.rearrange("(p j) w -> p j w", j=PACK))
+
+        k_scales = sb.tile([P, T], U8, name="k_scales", align_bytes=64)
+        scale_rows = keys_scales[0].bitcast(I32)
+        for quad in range(4):
+            nc.scalar.dma_start(
+                out=k_scales[32 * quad : 32 * quad + 4, :].bitcast(I32),
+                in_=scale_rows[4 * quad : 4 * quad + 4, :],
+            )
+
+        words = keys_words[0].rearrange("p n t -> p (n t)").bitcast(I32)
+        k_words = [sb.tile([P, half_t], U32, name="k_words%d" % h, align_bytes=64) for h in range(2)]
+        for h in range(2):
+            nc.sync.dma_start(out=k_words[h][:].bitcast(I32), in_=words[:, h * half_t : (h + 1) * half_t])
+
+        nc.sync.dma_start(idx2[:], offs2)
+        nc.sync.dma_start(idx3[:], offs3)
+        nc.sync.dma_start(idx1[:], offs)
+        lam_sb = sb.tile([P, 1], F32, name="lam_sb")
+        nc.sync.dma_start(out=lam_sb[:], in_=lam)
+        old_sb = sb.tile([P, T], F32, name="old_sb")
+        nc.sync.dma_start(out=old_sb[:], in_=old)
+        nc.sync.dma_start(idx4[:], offs4)
+
+        f1 = sb.tile([P, T], F32, name="f1")
+        nc.vector.memset(f1[:], 0.0)
+
+        q_bf = sb.tile([P, Q, PACK], BF16, name="q_bf", align_bytes=64)
+        nc.vector.tensor_copy(out=q_bf[:], in_=q_raw[:].rearrange("p j w -> p w j"))
+        q_words = sb.tile([P, Q], U32, name="q_words", align_bytes=64)
+        q_scales = sb.tile([P, Q], U8, name="q_scales", align_bytes=64)
+        nc.vector.quantize_mx(out=q_words[:].bitcast(FP8X4), scales=q_scales[:], in_=q_bf[:].rearrange("p w j -> p (w j)"))
+
+        a = sb.tile([P, T], F32, name="a")
+        for b in range(4):
+            bank = psum.tile([P, quarter_t], F32, name="bank%d" % b)
+            cols = slice(b * quarter_t, (b + 1) * quarter_t)
+            lo = (b % 2) * quarter_t
+            nc.tensor.matmul_mx(
+                out=bank[:],
+                lhsT=q_words[:].bitcast(FP8X4),
+                lhsT_scale=q_scales[:],
+                rhs=k_words[b // 2][:, lo : lo + quarter_t].bitcast(FP8X4),
+                rhs_scale=k_scales[:, cols],
+                start=True,
+                stop=True,
+            )
+            if b % 2 == 0:
+                nc.scalar.activation(a[:, cols], bank[:], COPY)
+            else:
+                nc.vector.tensor_copy(out=a[:, cols], in_=bank[:])
+
+        halves = [slice(c * half_i, (c + 1) * half_i) for c in range(2)]
+        list_halves = [slice(c * half_cols, (c + 1) * half_cols) for c in range(2)]
+        g1 = sb.tile([P, I], F32, name="g1")
+        g2 = [sb.tile([P, half_i], F32, name="g2_%d" % c) for c in range(2)]
+        g3 = [sb.tile([P, half_i], F32, name="g3_%d" % c) for c in range(2)]
+        larger = [sb.tile([P, half_i], F32, name="larger%d" % c) for c in range(2)]
+        lean = sb.tile([P, I], F32, name="lean")
+        for c in range(2):
+            nc.scalar.activation(g2[c][:], a[:].indirect(idx2[:, list_halves[c]]), COPY)
+            nc.vector.tensor_copy(g3[c][:], a[:].indirect(idx3[:, list_halves[c]]))
+        nc.scalar.activation(g1[:], a[:].indirect(idx1[:]), COPY)
+        for c in range(2):
+            nc.vector.tensor_tensor(larger[c][:], g2[c][:], g3[c][:], ALU.max)
+        for c in range(2):
+            nc.vector.tensor_scalar(lean[:, halves[c]], larger[c][:], lam_sb[:], None, ALU.mult)
+        nc.vector.tensor_tensor(f1[:].indirect(idx1[:]), g1[:], lean[:], ALU.add)
+
+        f2 = sb.tile([P, T], F32, name="f2")
+        nc.vector.tensor_tensor(f2[:], f1[:], old_sb[:], ALU.add)
+
+        y0 = sb.tile([P, half_i], F32, name="y0")
+        y1 = sb.tile([P, half_i], F32, name="y1")
+        nc.vector.tensor_copy(y0[:], f2[:].indirect(idx4[:, 0:half_cols]))
+        nc.sync.dma_start(out=out[:, 0:half_i], in_=y0[:])
+        nc.scalar.activation(y1[:], f2[:].indirect(idx4[:, half_cols:LIST_COLS]), COPY)
+        nc.scalar.dma_start(out=out[:, half_i:I], in_=y1[:])

@@ -23,7 +23,6 @@ LIST_COLS = I // 16
 def tile_attend_lookahead_lean_through_heads_kernel(tc, query, keys_words, keys_scales, lam, old, offs, offs2, offs3, offs4, out):
     nc = tc.nc
     half_t = T // 2
-    quarter_t = T // 4
     half_i = I // 2
     half_cols = LIST_COLS // 2
 
@@ -40,24 +39,23 @@ def tile_attend_lookahead_lean_through_heads_kernel(tc, query, keys_words, keys_
         q_raw = sb.tile([P, PACK, Q], F32, name="q_raw")
         nc.sync.dma_start(out=q_raw[:], in_=query.rearrange("(p j) w -> p j w", j=PACK))
 
+        words = keys_words[0].rearrange("p n t -> p (n t)").bitcast(I32)
+        k_words = [sb.tile([P, half_t], U32, name="k_words%d" % h, align_bytes=64) for h in range(2)]
         k_scales = sb.tile([P, T], U8, name="k_scales", align_bytes=64)
         scale_rows = keys_scales[0].bitcast(I32)
+        nc.sync.dma_start(out=k_words[0][:].bitcast(I32), in_=words[:, 0:half_t])
         for quad in range(4):
-            nc.scalar.dma_start(
+            nc.sync.dma_start(
                 out=k_scales[32 * quad : 32 * quad + 4, :].bitcast(I32),
                 in_=scale_rows[4 * quad : 4 * quad + 4, :],
             )
+        nc.sync.dma_start(out=k_words[1][:].bitcast(I32), in_=words[:, half_t:T])
 
-        words = keys_words[0].rearrange("p n t -> p (n t)").bitcast(I32)
-        k_words = [sb.tile([P, half_t], U32, name="k_words%d" % h, align_bytes=64) for h in range(2)]
-        for h in range(2):
-            nc.sync.dma_start(out=k_words[h][:].bitcast(I32), in_=words[:, h * half_t : (h + 1) * half_t])
-
+        lam_sb = sb.tile([P, 1], F32, name="lam_sb")
+        nc.sync.dma_start(out=lam_sb[:], in_=lam)
         nc.sync.dma_start(idx2[:], offs2)
         nc.sync.dma_start(idx3[:], offs3)
         nc.sync.dma_start(idx1[:], offs)
-        lam_sb = sb.tile([P, 1], F32, name="lam_sb")
-        nc.sync.dma_start(out=lam_sb[:], in_=lam)
         old_sb = sb.tile([P, T], F32, name="old_sb")
         nc.sync.dma_start(out=old_sb[:], in_=old)
         nc.sync.dma_start(idx4[:], offs4)
@@ -66,46 +64,53 @@ def tile_attend_lookahead_lean_through_heads_kernel(tc, query, keys_words, keys_
         nc.vector.memset(f1[:], 0.0)
 
         q_bf = sb.tile([P, Q, PACK], BF16, name="q_bf", align_bytes=64)
-        nc.vector.tensor_copy(out=q_bf[:], in_=q_raw[:].rearrange("p j w -> p w j"))
+        src = q_raw[:].rearrange("p j (c i) -> p c j i", i=4)
+        dst = q_bf[:].rearrange("p (c i) j -> p c j i", i=4)
+        runs = 22
+        nc.vector.tensor_copy(out=dst[:, 0:runs], in_=src[:, 0:runs])
+        nc.scalar.activation(dst[:, runs : Q // 4], src[:, runs : Q // 4], COPY)
         q_words = sb.tile([P, Q], U32, name="q_words", align_bytes=64)
         q_scales = sb.tile([P, Q], U8, name="q_scales", align_bytes=64)
         nc.vector.quantize_mx(out=q_words[:].bitcast(FP8X4), scales=q_scales[:], in_=q_bf[:].rearrange("p w j -> p (w j)"))
 
         a = sb.tile([P, T], F32, name="a")
-        for b in range(4):
-            bank = psum.tile([P, quarter_t], F32, name="bank%d" % b)
-            cols = slice(b * quarter_t, (b + 1) * quarter_t)
-            lo = (b % 2) * quarter_t
+        start = 0
+        for b, width in enumerate((256, 256, 256, 128, 128)):
+            bank = psum.tile([P, width], F32, name="bank%d" % b)
+            cols = slice(start, start + width)
+            lo = start % half_t
             nc.tensor.matmul_mx(
                 out=bank[:],
                 lhsT=q_words[:].bitcast(FP8X4),
                 lhsT_scale=q_scales[:],
-                rhs=k_words[b // 2][:, lo : lo + quarter_t].bitcast(FP8X4),
+                rhs=k_words[start // half_t][:, lo : lo + width].bitcast(FP8X4),
                 rhs_scale=k_scales[:, cols],
                 start=True,
                 stop=True,
             )
-            if b % 2 == 0:
+            if b % 2 == 1:
                 nc.scalar.activation(a[:, cols], bank[:], COPY)
             else:
                 nc.vector.tensor_copy(out=a[:, cols], in_=bank[:])
+            start += width
 
-        halves = [slice(c * half_i, (c + 1) * half_i) for c in range(2)]
         list_halves = [slice(c * half_cols, (c + 1) * half_cols) for c in range(2)]
-        g1 = sb.tile([P, I], F32, name="g1")
+        g1 = [sb.tile([P, half_i], F32, name="g1_%d" % c) for c in range(2)]
         g2 = [sb.tile([P, half_i], F32, name="g2_%d" % c) for c in range(2)]
         g3 = [sb.tile([P, half_i], F32, name="g3_%d" % c) for c in range(2)]
         larger = [sb.tile([P, half_i], F32, name="larger%d" % c) for c in range(2)]
-        lean = sb.tile([P, I], F32, name="lean")
+        lean = [sb.tile([P, half_i], F32, name="lean%d" % c) for c in range(2)]
         for c in range(2):
             nc.scalar.activation(g2[c][:], a[:].indirect(idx2[:, list_halves[c]]), COPY)
             nc.vector.tensor_copy(g3[c][:], a[:].indirect(idx3[:, list_halves[c]]))
-        nc.scalar.activation(g1[:], a[:].indirect(idx1[:]), COPY)
+        for c in range(2):
+            nc.scalar.activation(g1[c][:], a[:].indirect(idx1[:, list_halves[c]]), COPY)
         for c in range(2):
             nc.vector.tensor_tensor(larger[c][:], g2[c][:], g3[c][:], ALU.max)
         for c in range(2):
-            nc.vector.tensor_scalar(lean[:, halves[c]], larger[c][:], lam_sb[:], None, ALU.mult)
-        nc.vector.tensor_tensor(f1[:].indirect(idx1[:]), g1[:], lean[:], ALU.add)
+            nc.vector.tensor_scalar(lean[c][:], larger[c][:], lam_sb[:], None, ALU.mult)
+        for c in range(2):
+            nc.vector.tensor_tensor(f1[:].indirect(idx1[:, list_halves[c]]), g1[c][:], lean[c][:], ALU.add)
 
         f2 = sb.tile([P, T], F32, name="f2")
         nc.vector.tensor_tensor(f2[:], f1[:], old_sb[:], ALU.add)

@@ -1,6 +1,7 @@
 from contextlib import ExitStack
 
 import concourse.mybir as mybir
+from concourse.masks import make_identity
 
 D, T, I, Q = 512, 1024, 512, 128
 FLOPS = 2 * D * Q * T
@@ -45,23 +46,27 @@ def tile_attend_lookahead_lean_through_heads_kernel(tc, query, keys_words, keys_
         scale_rows = keys_scales[0].bitcast(I32)
         nc.sync.dma_start(out=k_words[0][:].bitcast(I32), in_=words[:, 0:half_t])
         for quad in range(4):
-            nc.sync.dma_start(
+            queue = nc.scalar if quad < 2 else nc.sync
+            queue.dma_start(
                 out=k_scales[32 * quad : 32 * quad + 4, :].bitcast(I32),
                 in_=scale_rows[4 * quad : 4 * quad + 4, :],
             )
         nc.sync.dma_start(out=k_words[1][:].bitcast(I32), in_=words[:, half_t:T])
 
-        lam_sb = sb.tile([P, 1], F32, name="lam_sb")
-        nc.sync.dma_start(out=lam_sb[:], in_=lam)
         nc.sync.dma_start(idx2[:], offs2)
         nc.sync.dma_start(idx3[:], offs3)
         nc.sync.dma_start(idx1[:], offs)
+        lam_sb = sb.tile([P, 1], F32, name="lam_sb")
+        nc.sync.dma_start(out=lam_sb[:], in_=lam)
         old_sb = sb.tile([P, T], F32, name="old_sb")
         nc.sync.dma_start(out=old_sb[:], in_=old)
         nc.sync.dma_start(idx4[:], offs4)
 
         f1 = sb.tile([P, T], F32, name="f1")
         nc.vector.memset(f1[:], 0.0)
+
+        ident = sb.tile([P, P], F32, name="ident")
+        make_identity(nc, ident[:])
 
         q_bf = sb.tile([P, Q, PACK], BF16, name="q_bf", align_bytes=64)
         src = q_raw[:].rearrange("p j (c i) -> p c j i", i=4)
@@ -75,8 +80,10 @@ def tile_attend_lookahead_lean_through_heads_kernel(tc, query, keys_words, keys_
 
         a = sb.tile([P, T], F32, name="a")
         start = 0
+        banks = []
         for b, width in enumerate((256, 256, 256, 128, 128)):
             bank = psum.tile([P, width], F32, name="bank%d" % b)
+            banks.append(bank)
             cols = slice(start, start + width)
             lo = start % half_t
             nc.tensor.matmul_mx(
@@ -113,7 +120,22 @@ def tile_attend_lookahead_lean_through_heads_kernel(tc, query, keys_words, keys_
             nc.vector.tensor_tensor(f1[:].indirect(idx1[:, list_halves[c]]), g1[c][:], lean[c][:], ALU.add)
 
         f2 = sb.tile([P, T], F32, name="f2")
-        nc.vector.tensor_tensor(f2[:], f1[:], old_sb[:], ALU.add)
+        turned = [g2[0], g2[1], g3[0]]
+        old_ps = [psum.tile([P, 4 * P], F32, name="old_ps0"), psum.tile([P, 2 * P], F32, name="old_ps1")]
+        for pair in range(3):
+            for u in range(2):
+                blk = 2 * pair + u
+                nc.tensor.transpose(banks[pair][:, u * P : (u + 1) * P], old_sb[:, blk * P : (blk + 1) * P], ident[:])
+            nc.scalar.activation(turned[pair][:], banks[pair][:], COPY)
+        for blk in range(6):
+            nc.tensor.transpose(
+                old_ps[blk // 4][:, (blk % 4) * P : (blk % 4 + 1) * P],
+                turned[blk // 2][:, (blk % 2) * P : (blk % 2 + 1) * P],
+                ident[:],
+            )
+        nc.gpsimd.tensor_tensor(f2[:, 6 * P : T], f1[:, 6 * P : T], old_sb[:, 6 * P : T], ALU.add)
+        nc.vector.tensor_tensor(f2[:, 0 : 4 * P], f1[:, 0 : 4 * P], old_ps[0][:], ALU.add)
+        nc.vector.tensor_tensor(f2[:, 4 * P : 6 * P], f1[:, 4 * P : 6 * P], old_ps[1][:], ALU.add)
 
         y0 = sb.tile([P, half_i], F32, name="y0")
         y1 = sb.tile([P, half_i], F32, name="y1")

from contextlib import ExitStack

import concourse.mybir as mybir
from concourse.masks import make_identity

D, T, I, Q = 512, 1024, 512, 128
FLOPS = 2 * D * Q * T

F32 = mybir.dt.float32
BF16 = mybir.dt.bfloat16
I32 = mybir.dt.int32
U32 = mybir.dt.uint32
U16 = mybir.dt.uint16
U8 = mybir.dt.uint8
FP8X4 = mybir.dt.float8_e4m3fn_x4
ALU = mybir.AluOpType
COPY = mybir.ActivationFunctionType.Copy

P = 128
PACK = 4
LIST_COLS = I // 16


def tile_attend_lookahead_lean_through_heads_kernel(tc, query, keys_words, keys_scales, lam, old, offs, offs2, offs3, offs4, out):
    nc = tc.nc
    half_t = T // 2
    half_i = I // 2
    half_cols = LIST_COLS // 2

    with ExitStack() as ctx:
        lists = ctx.enter_context(tc.tile_pool(name="lists", bufs=1))
        sb = ctx.enter_context(tc.tile_pool(name="sb", bufs=1))
        psum = ctx.enter_context(tc.psum_pool(name="psum", bufs=1))

        idx1 = lists.tile([P, LIST_COLS], U16, name="idx1")
        idx2 = lists.tile([P, LIST_COLS], U16, name="idx2")
        idx3 = lists.tile([P, LIST_COLS], U16, name="idx3")
        idx4 = lists.tile([P, LIST_COLS], U16, name="idx4")

        q_raw = sb.tile([P, PACK, Q], F32, name="q_raw")
        nc.sync.dma_start(out=q_raw[:], in_=query.rearrange("(p j) w -> p j w", j=PACK))

        words = keys_words[0].rearrange("p n t -> p (n t)").bitcast(I32)
        k_words = [sb.tile([P, half_t], U32, name="k_words%d" % h, align_bytes=64) for h in range(2)]
        k_scales = sb.tile([P, T], U8, name="k_scales", align_bytes=64)
        scale_rows = keys_scales[0].bitcast(I32)
        nc.sync.dma_start(out=k_words[0][:].bitcast(I32), in_=words[:, 0:half_t])
        for quad in range(4):
            queue = nc.scalar if quad < 2 else nc.sync
            queue.dma_start(
                out=k_scales[32 * quad : 32 * quad + 4, :].bitcast(I32),
                in_=scale_rows[4 * quad : 4 * quad + 4, :],
            )
        nc.sync.dma_start(out=k_words[1][:].bitcast(I32), in_=words[:, half_t:T])

        nc.sync.dma_start(idx2[:], offs2)
        nc.sync.dma_start(idx3[:], offs3)
        nc.sync.dma_start(idx1[:], offs)
        lam_sb = sb.tile([P, 1], F32, name="lam_sb")
        nc.sync.dma_start(out=lam_sb[:], in_=lam)
        old_sb = sb.tile([P, T], F32, name="old_sb")
        nc.sync.dma_start(out=old_sb[:], in_=old)
        nc.sync.dma_start(idx4[:], offs4)

        f1 = sb.tile([P, T], F32, name="f1")
        nc.vector.memset(f1[:], 0.0)

        ident = sb.tile([P, P], F32, name="ident")
        make_identity(nc, ident[:])

        q_bf = sb.tile([P, Q, PACK], BF16, name="q_bf", align_bytes=64)
        src = q_raw[:].rearrange("p j (c i) -> p c j i", i=4)
        dst = q_bf[:].rearrange("p (c i) j -> p c j i", i=4)
        runs = 22
        nc.vector.tensor_copy(out=dst[:, 0:runs], in_=src[:, 0:runs])
        nc.scalar.activation(dst[:, runs : Q // 4], src[:, runs : Q // 4], COPY)
        q_words = sb.tile([P, Q], U32, name="q_words", align_bytes=64)
        q_scales = sb.tile([P, Q], U8, name="q_scales", align_bytes=64)
        nc.vector.quantize_mx(out=q_words[:].bitcast(FP8X4), scales=q_scales[:], in_=q_bf[:].rearrange("p w j -> p (w j)"))

        a = sb.tile([P, T], F32, name="a")
        start = 0
        banks = []
        for b, width in enumerate((256, 256, 256, 128, 128)):
            bank = psum.tile([P, width], F32, name="bank%d" % b)
            banks.append(bank)
            cols = slice(start, start + width)
            lo = start % half_t
            nc.tensor.matmul_mx(
                out=bank[:],
                lhsT=q_words[:].bitcast(FP8X4),
                lhsT_scale=q_scales[:],
                rhs=k_words[start // half_t][:, lo : lo + width].bitcast(FP8X4),
                rhs_scale=k_scales[:, cols],
                start=True,
                stop=True,
            )
            if b % 2 == 1:
                nc.scalar.activation(a[:, cols], bank[:], COPY)
            else:
                nc.vector.tensor_copy(out=a[:, cols], in_=bank[:])
            start += width

        list_halves = [slice(c * half_cols, (c + 1) * half_cols) for c in range(2)]
        g1 = [sb.tile([P, half_i], F32, name="g1_%d" % c) for c in range(2)]
        g2 = [sb.tile([P, half_i], F32, name="g2_%d" % c) for c in range(2)]
        g3 = [sb.tile([P, half_i], F32, name="g3_%d" % c) for c in range(2)]
        larger = [sb.tile([P, half_i], F32, name="larger%d" % c) for c in range(2)]
        lean = [sb.tile([P, half_i], F32, name="lean%d" % c) for c in range(2)]
        for c in range(2):
            nc.scalar.activation(g2[c][:], a[:].indirect(idx2[:, list_halves[c]]), COPY)
            nc.vector.tensor_copy(g3[c][:], a[:].indirect(idx3[:, list_halves[c]]))
        for c in range(2):
            nc.scalar.activation(g1[c][:], a[:].indirect(idx1[:, list_halves[c]]), COPY)
        for c in range(2):
            nc.vector.tensor_tensor(larger[c][:], g2[c][:], g3[c][:], ALU.max)
        for c in range(2):
            nc.vector.tensor_scalar(lean[c][:], larger[c][:], lam_sb[:], None, ALU.mult)
        for c in range(2):
            nc.vector.tensor_tensor(f1[:].indirect(idx1[:, list_halves[c]]), g1[c][:], lean[c][:], ALU.add)

        f2 = sb.tile([P, T], F32, name="f2")
        turned = [g2[0], g2[1], g3[0]]
        old_ps = [psum.tile([P, 4 * P], F32, name="old_ps0"), psum.tile([P, 2 * P], F32, name="old_ps1")]
        for pair in range(3):
            for u in range(2):
                blk = 2 * pair + u
                nc.tensor.transpose(banks[pair][:, u * P : (u + 1) * P], old_sb[:, blk * P : (blk + 1) * P], ident[:])
            nc.scalar.activation(turned[pair][:], banks[pair][:], COPY)
        for blk in range(6):
            nc.tensor.transpose(
                old_ps[blk // 4][:, (blk % 4) * P : (blk % 4 + 1) * P],
                turned[blk // 2][:, (blk % 2) * P : (blk % 2 + 1) * P],
                ident[:],
            )
        nc.gpsimd.tensor_tensor(f2[:, 6 * P : T], f1[:, 6 * P : T], old_sb[:, 6 * P : T], ALU.add)
        nc.vector.tensor_tensor(f2[:, 0 : 4 * P], f1[:, 0 : 4 * P], old_ps[0][:], ALU.add)
        nc.vector.tensor_tensor(f2[:, 4 * P : 6 * P], f1[:, 4 * P : 6 * P], old_ps[1][:], ALU.add)

        y0 = sb.tile([P, half_i], F32, name="y0")
        y1 = sb.tile([P, half_i], F32, name="y1")
        nc.vector.tensor_copy(y0[:], f2[:].indirect(idx4[:, 0:half_cols]))
        nc.sync.dma_start(out=out[:, 0:half_i], in_=y0[:])
        nc.scalar.activation(y1[:], f2[:].indirect(idx4[:, half_cols:LIST_COLS]), COPY)
        nc.scalar.dma_start(out=out[:, half_i:I], in_=y1[:])
